import numpy as np
import ml_dtypes


def mxq(x, axis, fmt="e4m3"):
    dtype, down = {"e4m3": (ml_dtypes.float8_e4m3fn, 7), "e5m2": (ml_dtypes.float8_e5m2, 14)}[fmt]
    v = np.moveaxis(np.asarray(x, np.float32).astype(ml_dtypes.bfloat16).astype(np.float64), axis, -1)
    blocks = v.reshape(v.shape[:-1] + (-1, 32))
    amax = np.abs(blocks).max(-1, keepdims=True)
    byte = np.maximum(np.where(amax > 0, np.frexp(amax)[1] - 1 + 127, 0) - down, 1)
    scale = np.exp2(byte - 127.0)
    codes = (blocks / scale).astype(np.float32).astype(dtype).astype(np.float64)
    return np.moveaxis((codes * scale).reshape(v.shape), -1, axis)


WIDE = False


def mx_kscale(k):
    if not WIDE:
        return np.ones(k)
    levels = np.array([10, -10, 5, -5, 0])
    if k % 512:
        return np.exp2(np.random.permutation(np.resize(levels, k // 32))).repeat(32)
    a = np.empty((k // 512, 16))
    for p in range(k // 512):
        a[p, :8] = np.random.permutation(np.resize(levels, 8))
        for g in range(8):
            far = levels[np.abs(levels - a[p, g]) >= 10]
            a[p, g + 8] = far[np.random.randint(len(far))]
    return np.exp2(a.ravel()).repeat(32)


def f64(x):
    return np.asarray(x).astype(np.float64)


def striped(idx):
    return np.tile(np.asarray(idx).reshape(-1, 16).T, (8, 1)).astype(np.uint16)


def unstriped(offs):
    return offs[:16].T.reshape(-1).astype(np.int64)


E2M1 = np.array([0.0, 0.5, 1.0, 1.5, 2.0, 3.0, 4.0, 6.0, -0.0, -0.5, -1.0, -1.5, -2.0, -3.0, -4.0, -6.0])


def pack_weight(w, fmt):
    k, n = w.shape
    w = f64(np.asarray(w, np.float32).astype(ml_dtypes.bfloat16)).reshape(k // 32, 32, n)
    amax = np.abs(w).max(1)
    if fmt == "e4m3":
        byte = np.frexp(amax)[1] - 1 + 127 - 7
    else:
        mant, ex = np.frexp(amax / 6.0)
        byte = np.where(mant > 0.5, ex, ex - 1) + 127
    byte = np.clip(np.where(amax > 0, byte, 1), 1, 254)
    scaled = (w * np.exp2(127.0 - byte)[:, None, :]).reshape(k, n).astype(np.float32)
    by_word = np.ascontiguousarray(scaled.reshape(k // 512, 128, 4, n).transpose(0, 1, 3, 2))
    if fmt == "e4m3":
        words = by_word.astype(ml_dtypes.float8_e4m3fn).view(np.uint8)
    else:
        c = by_word.astype(ml_dtypes.float4_e2m1fn).view(np.uint8) & 0xF
        words = (c[..., 0::2] | (c[..., 1::2] << 4)).reshape(k // 512, 128, 2 * n)
    return np.ascontiguousarray(words), np.ascontiguousarray(byte.astype(np.uint8).reshape(k // 512, 16, n))


def unpack_weight(words, scales, fmt):
    g, _, n = scales.shape
    words = np.ascontiguousarray(words).reshape(g, 128, n, -1)
    if fmt == "e4m3":
        vals = words.view(ml_dtypes.float8_e4m3fn).astype(np.float64)
    else:
        nib = np.empty((g, 128, n, 4), np.uint8)
        nib[..., 0::2] = words & 0xF
        nib[..., 1::2] = words >> 4
        vals = E2M1[nib]
    vals = vals * np.repeat(np.exp2(scales.astype(np.float64) - 127.0), 8, axis=1)[..., None]
    return vals.transpose(0, 1, 3, 2).reshape(g * 512, n)


D, E, T, I, Q = 512, 512, 2048, 512, 128


def setup_inputs():
    n = np.random.standard_normal
    idx2 = np.random.permutation(I)[:I]
    idx = np.random.permutation(T)[:I]
    fd = mx_kscale(D)
    fi = mx_kscale(I)
    ti = np.ones(T)
    ti[idx] = fi
    keysp = pack_weight(n((D, T)) / fd[:, None], "e2m1")
    return {
        "query": (n((D, Q)) * 0.8 / np.sqrt(D) * fd[:, None]).astype(np.float32),
        "keys_words": keysp[0],
        "keys_scales": keysp[1],
        "reserve": (np.random.uniform(0.5, 2.0, (Q, 1))).astype(np.float32),
        "dquery": (n((D, Q)) * 0.6 / np.sqrt(D) * fd[:, None]).astype(np.float32),
        "os": (np.random.uniform(4.0, 16.0, (1, I)) * fi).astype(np.float32),
        "vals": (n((E, T)) / ti).astype(np.float32),
        "offs2": striped(idx2),
        "offs": striped(idx),
    }


def reference(query, keys_words, keys_scales, reserve, dquery, os, vals, offs2, offs):
    idx2 = unstriped(offs2)
    idx = unstriped(offs)
    keysu = unpack_weight(keys_words, keys_scales, "e2m1")
    queryq = mxq(f64(query), 0, "e4m3")
    keysidxg = keysu[:, idx]
    a = queryq.T @ keysidxg
    dqueryq = mxq(f64(dquery), 0, "e4m3")
    ta = dqueryq.T @ keysidxg
    p = np.exp(a)
    z = np.sum(p, axis=1, keepdims=True)
    r = p / (p + p[:, idx2] + f64(reserve))
    tp = ta * p
    tz = np.sum(tp, axis=1, keepdims=True)
    tr = (tp - (tp + tp[:, idx2]) * p / (p + p[:, idx2] + f64(reserve))) / (p + p[:, idx2] + f64(reserve))
    tw = (tp - tz * p / z) / z * r + tr * p / z
    wo1 = tw * f64(os)
    wt1 = wo1.T
    vt1 = f64(vals)[:, idx].T
    wt1q = mxq(wt1, 0, "e4m3")
    vt1q = mxq(vt1, 0, "e4m3")
    o = wt1q.T @ vt1q
    return o

@@ -1,0 +1,199 @@
+from contextlib import ExitStack
+
+import concourse.mybir as mybir
+from concourse.masks import make_identity
+
+F32 = mybir.dt.float32
+BF16 = mybir.dt.bfloat16
+I32 = mybir.dt.int32
+U32 = mybir.dt.uint32
+U16 = mybir.dt.uint16
+U8 = mybir.dt.uint8
+FP8X4 = mybir.dt.float8_e4m3fn_x4
+FP4X4 = mybir.dt.float4_e2m1fn_x4
+ALU = mybir.AluOpType
+ACT = mybir.ActivationFunctionType
+AX = mybir.AxisListType
+
+P = 128
+D, E, T, I, Q = 512, 512, 2048, 512, 128
+PACK = 4
+SPARE = 16
+SHIFT_LIMIT = 80.0
+FLOPS = 2 * Q * I * D * 2 + 2 * Q * E * I
+
+
+def tile_attend_ttneighbourshare_kernel(tc, query, keys_words, keys_scales, reserve, dquery, slot_factor, vals, offs2, offs, out):
+    nc = tc.nc
+    with ExitStack() as ctx:
+        keep = ctx.enter_context(tc.tile_pool(name="keep", bufs=1))
+        psum = ctx.enter_context(tc.psum_pool(name="psum", bufs=1))
+        turn = ctx.enter_context(tc.psum_pool(name="turn", bufs=2))
+
+        def sb(shape, dtype, name, tag=None):
+            return keep.tile(shape, dtype, name=name, tag=tag or name, align_bytes=64)
+
+        idx = keep.tile([P, I // 16], U16, name="idx")
+        idx2 = keep.tile([P, I // 16], U16, name="idx2")
+        kscale_pool = sb([P, T], U8, "kscale_pool")
+        kword_pool = sb([P, T], U16, "kword_pool")
+        q_raw = sb([P, PACK, Q], F32, "q_raw")
+        dq_raw = sb([P, PACK, Q], F32, "dq_raw")
+        v_pool = [sb([P, T], F32, "v_pool%d" % b) for b in range(E // P)]
+        res_col = sb([P, 1], F32, "res_col")
+        os_col = sb([P, PACK], F32, "os_col")
+
+        nc.gpsimd.memset(kscale_pool[:].bitcast(I32), 0)
+        nc.sync.dma_start(idx[:], offs)
+        nc.sync.dma_start(os_col[:], slot_factor.rearrange("o (p j) -> (o p) j", j=PACK))
+        for quad in range(4):
+            nc.sync.dma_start(
+                kscale_pool[32 * quad : 32 * quad + 4, :].bitcast(I32),
+                keys_scales[0, 4 * quad : 4 * quad + 4, :].bitcast(I32),
+            )
+        nc.sync.dma_start(kword_pool[:].bitcast(I32), keys_words[0].bitcast(I32))
+        nc.sync.dma_start(q_raw[:], query.rearrange("(p j) c -> p j c", j=PACK))
+        nc.sync.dma_start(dq_raw[:], dquery.rearrange("(p j) c -> p j c", j=PACK))
+        nc.sync.dma_start(v_pool[0][:], vals[0:P, :])
+        nc.sync.dma_start(res_col[:], reserve)
+        nc.sync.dma_start(idx2[:], offs2)
+        for b in range(1, E // P):
+            nc.sync.dma_start(v_pool[b][:], vals[b * P : (b + 1) * P, :])
+
+        ident = sb([P, P], F32, "ident")
+        make_identity(nc, ident[:])
+        p_win = sb([P, I + SPARE * 12], F32, "p_win")
+        tp_win = sb([P, I + SPARE * 12], F32, "tp_win")
+        nc.gpsimd.memset(p_win[:, I:], 0.0)
+        nc.gpsimd.memset(tp_win[:, I:], 0.0)
+        p = p_win[:, 0:I]
+        tp = tp_win[:, 0:I]
+
+        kscales = sb([P, I], U8, "kscales")
+        nc.vector.tensor_copy(kscales[:], kscale_pool[:].indirect(idx[:]))
+        kwords = sb([P, I], U16, "kwords", "kscale_pool")
+        nc.vector.tensor_copy(kwords[:], kword_pool[:].indirect(idx[:]))
+
+        def scores(raw, name):
+            grouped = sb([P, Q, PACK], BF16, name + "_grouped")
+            codes = sb([P, Q], U32, name + "_codes")
+            scales = sb([P, Q], U8, name + "_scales")
+            acc = psum.tile([P, I], F32, name=name + "_acc")
+            nc.scalar.copy(grouped[:], raw[:].rearrange("p j c -> p c j"))
+            nc.vector.quantize_mx(out=codes[:].bitcast(FP8X4), scales=scales[:], in_=grouped[:].rearrange("p c j -> p (c j)"))
+            nc.tensor.matmul_mx(
+                out=acc[:], lhsT=codes[:].bitcast(FP8X4), lhsT_scale=scales[:],
+                rhs=kwords[:].bitcast(FP4X4), rhs_scale=kscales[:], start=True, stop=True,
+            )
+            return acc
+
+        a = scores(q_raw, "q")
+        ta = scores(dq_raw, "dq")
+
+        os_ps = psum.tile([P, PACK, P], F32, name="os_ps")
+        for j in range(PACK):
+            nc.tensor.transpose(os_ps[:, j, :], os_col[:, j : j + 1].to_broadcast([P, P]), ident[:])
+        os_row = sb([P, I], F32, "os_row")
+        nc.scalar.copy(os_row[:].rearrange("q (n j) -> q n j", j=PACK), os_ps[:].rearrange("q j n -> q n j"))
+
+        neg_max = sb([P, 1], F32, "neg_max")
+        neg_lim = sb([P, 1], F32, "neg_lim")
+        shrink = sb([P, 1], F32, "shrink")
+        res_sh = sb([P, 1], F32, "res_sh")
+        z = sb([P, 1], F32, "z")
+        tz = sb([P, 1], F32, "tz")
+        rz = sb([P, 1], F32, "rz")
+        c = sb([P, 1], F32, "c")
+        nc.vector.tensor_reduce(neg_max[:], a[:], AX.X, ALU.max, negate=True)
+        nc.vector.tensor_scalar(neg_lim[:], neg_max[:], SHIFT_LIMIT, -SHIFT_LIMIT, ALU.min, ALU.max)
+        nc.scalar.activation(p, a[:], ACT.Exp, bias=neg_max[:], accum_out=z[:])
+        nc.scalar.activation(shrink[:], neg_lim[:], ACT.Exp)
+        nc.scalar.activation(res_sh[:], shrink[:], ACT.Copy, scale=res_col[:])
+
+        def turn_and_quantize(src, name, grouped_tag=None, codes_tag=None):
+            words = src[:].bitcast(F32)
+            turned = turn.tile([P, 2, P], F32, name="turned")
+            for h in range(2):
+                nc.tensor.transpose(turned[:, h, :], words[:, h : I // 2 : 2], ident[:])
+            grouped = sb([P, P * PACK], BF16, name + "_grouped", grouped_tag)
+            codes = sb([P, P], U32, name + "_codes", codes_tag)
+            scales = sb([P, P], U8, name + "_scales")
+            nc.scalar.copy(
+                grouped[:].bitcast(F32).rearrange("p (c h) -> p c h", h=2), turned[:].rearrange("p h c -> p c h")
+            )
+            nc.vector.quantize_mx(out=codes[:].bitcast(FP8X4), scales=scales[:], in_=grouped[:])
+            return codes, scales
+
+        def pick_on_vector(b, tag=None):
+            picked = sb([P, I], BF16, "picked%d" % b, tag)
+            nc.vector.tensor_copy(picked[:], v_pool[b][:].indirect(idx[:]))
+            return picked
+
+        picked0 = pick_on_vector(0)
+
+        p2 = sb([P, I], F32, "p2", "v_pool0")
+        pair = sb([P, I], F32, "pair")
+        tp2 = sb([P, I], F32, "tp2")
+        psq = sb([P, I], F32, "psq")
+        nc.vector.tensor_copy(p2[:], p_win[:].indirect(idx2[:]))
+        nc.vector.scalar_tensor_tensor(tp, ta[:], 1.0, p, ALU.mult, ALU.mult, accum_out=tz[:])
+        nc.vector.tensor_tensor(pair[:], p2[:], p, ALU.add)
+        nc.vector.tensor_copy(tp2[:], tp_win[:].indirect(idx2[:]))
+        nc.vector.reciprocal(rz[:], z[:])
+        nc.vector.tensor_scalar(c[:], tz[:], rz[:], 0.5, ALU.mult, ALU.mult)
+
+        root = sb([P, I], F32, "root")
+        rabs = sb([P, I], F32, "rabs")
+        sgn = sb([P, I], F32, "sgn")
+        nc.scalar.activation(psq[:], p, ACT.Square)
+        v_mx = [turn_and_quantize(picked0, "v0")]
+        nc.scalar.activation(root[:], pair[:], ACT.Abs_reciprocal_sqrt, bias=res_sh[:])
+        nc.scalar.activation(rabs[:], root[:], ACT.Square)
+        nc.scalar.activation(sgn[:], pair[:], ACT.Sign, bias=res_sh[:])
+
+        g = sb([P, I], F32, "g", "v_pool0")
+        u = sb([P, I], F32, "u")
+        nc.gpsimd.tensor_tensor(g[:], psq[:], os_row[:], ALU.mult)
+        nc.gpsimd.tensor_tensor(u[:], tp2[:], tp, ALU.add)
+
+        picked1 = pick_on_vector(1)
+
+        aa = sb([P, I], F32, "aa", "v_pool1")
+        bb = sb([P, I], F32, "bb")
+        ee = sb([P, I], F32, "ee")
+        ff = sb([P, I], F32, "ff")
+        w = sb([P, I], BF16, "w")
+        nc.vector.scalar_tensor_tensor(aa[:], ta[:], c[:], sgn[:], ALU.subtract, ALU.mult)
+        nc.vector.scalar_tensor_tensor(bb[:], u[:], 0.5, rabs[:], ALU.mult, ALU.mult)
+        nc.vector.scalar_tensor_tensor(ff[:], g[:], rz[:], rabs[:], ALU.mult, ALU.mult)
+        halves = [slice(0, I // 2), slice(I // 2, I)]
+        for h in halves:
+            nc.vector.tensor_tensor(ee[:, h], aa[:, h], bb[:, h], ALU.subtract)
+        for h in halves:
+            nc.vector.scalar_tensor_tensor(w[:, h], ee[:, h], 2.0, ff[:, h], ALU.mult, ALU.mult)
+
+        cast = sb([P, T], BF16, "cast", "pair")
+        picked2 = sb([P, I], BF16, "picked2")
+        nc.scalar.activation(cast[:], v_pool[2][:], ACT.Copy)
+        v_mx.append(turn_and_quantize(picked1, "v1", "v_pool2", "ff"))
+        nc.scalar.activation(picked2[:], cast[:].indirect(idx[:]), ACT.Copy)
+        picked3 = pick_on_vector(3, "ee")
+        w_codes, w_scales = turn_and_quantize(w, "w")
+        v_mx.append(turn_and_quantize(picked2, "v2"))
+        v_mx.append(turn_and_quantize(picked3, "v3"))
+
+        def product(blocks, name, evacuate):
+            width = len(blocks) * P
+            acc = psum.tile([P, width], F32, name=name + "_acc")
+            for n, b in enumerate(blocks):
+                nc.tensor.matmul_mx(
+                    out=acc[:, n * P : (n + 1) * P], lhsT=w_codes[:].bitcast(FP8X4), lhsT_scale=w_scales[:],
+                    rhs=v_mx[b][0][:].bitcast(FP8X4), rhs_scale=v_mx[b][1][:], start=True, stop=True,
+                )
+            staged = sb([P, width], F32, name + "_staged")
+            evacuate(staged[:], acc[:])
+            nc.sync.dma_start(out[:, blocks[0] * P : blocks[0] * P + width], staged[:])
+
+        product([0, 1], "out01", nc.vector.tensor_copy)
+        product([2], "out2", nc.scalar.copy)
+        product([3], "out3", nc.vector.tensor_copy)

@@ -20,6 +20,8 @@ D, E, T, I, Q = 512, 512, 2048, 512, 128
 PACK = 4
 SPARE = 16
 SHIFT_LIMIT = 80.0
+BLOCK = 4 * T
+ROW = 4 * I
 FLOPS = 2 * Q * I * D * 2 + 2 * Q * E * I
 
 
@@ -28,7 +30,11 @@ def tile_attend_ttneighbourshare_kernel(tc, query, keys_words, keys_scales, rese
     with ExitStack() as ctx:
         keep = ctx.enter_context(tc.tile_pool(name="keep", bufs=1))
         psum = ctx.enter_context(tc.psum_pool(name="psum", bufs=1))
-        turn = ctx.enter_context(tc.psum_pool(name="turn", bufs=2))
+
+        reuse = ctx.enter_context(tc.tile_pool(name="reuse", bufs=1))
+
+        def at(offset, shape, dtype, name):
+            return reuse.tile(shape, dtype, name=name, offset=offset, align_bytes=64)
 
         def sb(shape, dtype, name, tag=None):
             return keep.tile(shape, dtype, name=name, tag=tag or name, align_bytes=64)
@@ -39,88 +45,99 @@ def tile_attend_ttneighbourshare_kernel(tc, query, keys_words, keys_scales, rese
         kword_pool = sb([P, T], U16, "kword_pool")
         q_raw = sb([P, PACK, Q], F32, "q_raw")
         dq_raw = sb([P, PACK, Q], F32, "dq_raw")
-        v_pool = [sb([P, T], F32, "v_pool%d" % b) for b in range(E // P)]
+        v_pool = [at(b * BLOCK, [P, T], F32, "v_pool%d" % b) for b in range(E // P)]
         res_col = sb([P, 1], F32, "res_col")
         os_col = sb([P, PACK], F32, "os_col")
 
-        nc.gpsimd.memset(kscale_pool[:].bitcast(I32), 0)
+        nc.vector.memset(kscale_pool[:].bitcast(I32), 0)
         nc.sync.dma_start(idx[:], offs)
         nc.sync.dma_start(os_col[:], slot_factor.rearrange("o (p j) -> (o p) j", j=PACK))
+        nc.sync.dma_start(kword_pool[:].bitcast(I32), keys_words[0].bitcast(I32))
+        nc.sync.dma_start(q_raw[:], query.rearrange("(p j) c -> p j c", j=PACK))
         for quad in range(4):
             nc.sync.dma_start(
                 kscale_pool[32 * quad : 32 * quad + 4, :].bitcast(I32),
                 keys_scales[0, 4 * quad : 4 * quad + 4, :].bitcast(I32),
             )
-        nc.sync.dma_start(kword_pool[:].bitcast(I32), keys_words[0].bitcast(I32))
-        nc.sync.dma_start(q_raw[:], query.rearrange("(p j) c -> p j c", j=PACK))
         nc.sync.dma_start(dq_raw[:], dquery.rearrange("(p j) c -> p j c", j=PACK))
         nc.sync.dma_start(v_pool[0][:], vals[0:P, :])
-        nc.sync.dma_start(res_col[:], reserve)
         nc.sync.dma_start(idx2[:], offs2)
+        nc.sync.dma_start(res_col[:], reserve)
         for b in range(1, E // P):
             nc.sync.dma_start(v_pool[b][:], vals[b * P : (b + 1) * P, :])
 
         ident = sb([P, P], F32, "ident")
         make_identity(nc, ident[:])
         p_win = sb([P, I + SPARE * 12], F32, "p_win")
-        tp_win = sb([P, I + SPARE * 12], F32, "tp_win")
         nc.gpsimd.memset(p_win[:, I:], 0.0)
-        nc.gpsimd.memset(tp_win[:, I:], 0.0)
         p = p_win[:, 0:I]
-        tp = tp_win[:, 0:I]
 
-        kscales = sb([P, I], U8, "kscales")
-        nc.vector.tensor_copy(kscales[:], kscale_pool[:].indirect(idx[:]))
-        kwords = sb([P, I], U16, "kwords", "kscale_pool")
-        nc.vector.tensor_copy(kwords[:], kword_pool[:].indirect(idx[:]))
-
-        def scores(raw, name):
-            grouped = sb([P, Q, PACK], BF16, name + "_grouped")
-            codes = sb([P, Q], U32, name + "_codes")
-            scales = sb([P, Q], U8, name + "_scales")
-            acc = psum.tile([P, I], F32, name=name + "_acc")
-            nc.scalar.copy(grouped[:], raw[:].rearrange("p j c -> p c j"))
-            nc.vector.quantize_mx(out=codes[:].bitcast(FP8X4), scales=scales[:], in_=grouped[:].rearrange("p c j -> p (c j)"))
-            nc.tensor.matmul_mx(
-                out=acc[:], lhsT=codes[:].bitcast(FP8X4), lhsT_scale=scales[:],
-                rhs=kwords[:].bitcast(FP4X4), rhs_scale=kscales[:], start=True, stop=True,
-            )
-            return acc
-
-        a = scores(q_raw, "q")
-        ta = scores(dq_raw, "dq")
-
-        os_ps = psum.tile([P, PACK, P], F32, name="os_ps")
+        os_ps = psum.tile([P, PACK, P], F32, name="os_ps", tag="os_ps")
         for j in range(PACK):
             nc.tensor.transpose(os_ps[:, j, :], os_col[:, j : j + 1].to_broadcast([P, P]), ident[:])
         os_row = sb([P, I], F32, "os_row")
         nc.scalar.copy(os_row[:].rearrange("q (n j) -> q n j", j=PACK), os_ps[:].rearrange("q j n -> q n j"))
 
-        neg_max = sb([P, 1], F32, "neg_max")
+        halves = [slice(0, I // 2), slice(I // 2, I)]
+        list_halves = [slice(0, I // 32), slice(I // 32, I // 16)]
+
+        def quantize_rows(raw, name, codes_tag):
+            grouped = sb([P, Q, PACK], BF16, name + "_grouped")
+            codes = sb([P, Q], U32, name + "_codes", codes_tag)
+            scales = sb([P, Q], U8, name + "_scales")
+            nc.scalar.copy(grouped[:], raw[:].rearrange("p j c -> p c j"))
+            nc.vector.quantize_mx(out=codes[:].bitcast(FP8X4), scales=scales[:], in_=grouped[:].rearrange("p c j -> p (c j)"))
+            return codes, scales
+
+        kwords = sb([P, I], U16, "kwords")
+        nc.vector.tensor_copy(kwords[:], kword_pool[:].indirect(idx[:]))
+        kscales = [sb([P, I // 2], U8, "kscales0", "kword_pool")]
+        nc.vector.tensor_copy(kscales[0][:], kscale_pool[:].indirect(idx[:, list_halves[0]]))
+        q_mx = quantize_rows(q_raw, "q", "os_col")
+        kscales.append(sb([P, I // 2], U8, "kscales1", "q_grouped"))
+        nc.vector.tensor_copy(kscales[1][:], kscale_pool[:].indirect(idx[:, list_halves[1]]))
+        dq_mx = quantize_rows(dq_raw, "dq", "kscale_pool")
+
+        def scores(rows_mx, name):
+            acc = psum.tile([P, I], F32, name=name, tag=name)
+            for h in range(2):
+                nc.tensor.matmul_mx(
+                    out=acc[:, halves[h]], lhsT=rows_mx[0][:].bitcast(FP8X4), lhsT_scale=rows_mx[1][:],
+                    rhs=kwords[:, halves[h]].bitcast(FP4X4), rhs_scale=kscales[h][:], start=True, stop=True,
+                )
+            return acc
+
+        a = scores(q_mx, "a")
+        ta = scores(dq_mx, "ta")
+
+        neg_max = sb([P, 1], F32, "neg_max", "dq_grouped")
         neg_lim = sb([P, 1], F32, "neg_lim")
         shrink = sb([P, 1], F32, "shrink")
         res_sh = sb([P, 1], F32, "res_sh")
         z = sb([P, 1], F32, "z")
         tz = sb([P, 1], F32, "tz")
-        rz = sb([P, 1], F32, "rz")
         c = sb([P, 1], F32, "c")
         nc.vector.tensor_reduce(neg_max[:], a[:], AX.X, ALU.max, negate=True)
-        nc.vector.tensor_scalar(neg_lim[:], neg_max[:], SHIFT_LIMIT, -SHIFT_LIMIT, ALU.min, ALU.max)
+        nc.gpsimd.tensor_scalar(neg_lim[:], neg_max[:], SHIFT_LIMIT, -SHIFT_LIMIT, ALU.min, ALU.max)
         nc.scalar.activation(p, a[:], ACT.Exp, bias=neg_max[:], accum_out=z[:])
+        psq = sb([P, I], F32, "psq")
+        g = sb([P, I], F32, "g")
+        nc.scalar.activation(psq[:], p, ACT.Square)
+        nc.gpsimd.tensor_tensor(g[:], psq[:], os_row[:], ALU.mult)
         nc.scalar.activation(shrink[:], neg_lim[:], ACT.Exp)
         nc.scalar.activation(res_sh[:], shrink[:], ACT.Copy, scale=res_col[:])
 
-        def turn_and_quantize(src, name, grouped_tag=None, codes_tag=None):
+        def turn(src, name, bank, grouped, evacuate=nc.scalar.copy):
             words = src[:].bitcast(F32)
-            turned = turn.tile([P, 2, P], F32, name="turned")
+            turned = psum.tile([P, 2, P], F32, name=name + "_turned", tag=bank)
             for h in range(2):
                 nc.tensor.transpose(turned[:, h, :], words[:, h : I // 2 : 2], ident[:])
-            grouped = sb([P, P * PACK], BF16, name + "_grouped", grouped_tag)
-            codes = sb([P, P], U32, name + "_codes", codes_tag)
-            scales = sb([P, P], U8, name + "_scales")
-            nc.scalar.copy(
-                grouped[:].bitcast(F32).rearrange("p (c h) -> p c h", h=2), turned[:].rearrange("p h c -> p c h")
+            evacuate(
+                grouped.bitcast(F32).rearrange("p (c h) -> p c h", h=2), turned[:].rearrange("p h c -> p c h")
             )
+
+        def quantize(grouped, codes, name):
+            scales = sb([P, codes.shape[1]], U8, name + "_scales")
             nc.vector.quantize_mx(out=codes[:].bitcast(FP8X4), scales=scales[:], in_=grouped[:])
             return codes, scales
 
@@ -130,70 +147,78 @@ def tile_attend_ttneighbourshare_kernel(tc, query, keys_words, keys_scales, rese
             return picked
 
         picked0 = pick_on_vector(0)
+        v0_grouped = sb([P, I], BF16, "v0_grouped", "shrink")
+        turn(picked0, "v0", "turn0", v0_grouped[:])
 
-        p2 = sb([P, I], F32, "p2", "v_pool0")
-        pair = sb([P, I], F32, "pair")
+        p2 = at(0, [P, I], F32, "p2")
+        rz = at(ROW, [P, 1], F32, "rz")
+        tp_win = at(2 * ROW, [P, I + SPARE * 12], F32, "tp_win")
+        nc.gpsimd.memset(tp_win[:, I:], 0.0)
+        tp = tp_win[:, 0:I]
+        pair = sb([P, I], F32, "pair", "psq")
         tp2 = sb([P, I], F32, "tp2")
-        psq = sb([P, I], F32, "psq")
+        u = sb([P, I], F32, "u")
         nc.vector.tensor_copy(p2[:], p_win[:].indirect(idx2[:]))
         nc.vector.scalar_tensor_tensor(tp, ta[:], 1.0, p, ALU.mult, ALU.mult, accum_out=tz[:])
-        nc.vector.tensor_tensor(pair[:], p2[:], p, ALU.add)
+        nc.gpsimd.tensor_tensor(pair[:], p2[:], p, ALU.add)
         nc.vector.tensor_copy(tp2[:], tp_win[:].indirect(idx2[:]))
+        nc.gpsimd.tensor_tensor(u[:], tp2[:], tp, ALU.add)
         nc.vector.reciprocal(rz[:], z[:])
         nc.vector.tensor_scalar(c[:], tz[:], rz[:], 0.5, ALU.mult, ALU.mult)
 
         root = sb([P, I], F32, "root")
         rabs = sb([P, I], F32, "rabs")
         sgn = sb([P, I], F32, "sgn")
-        nc.scalar.activation(psq[:], p, ACT.Square)
-        v_mx = [turn_and_quantize(picked0, "v0")]
         nc.scalar.activation(root[:], pair[:], ACT.Abs_reciprocal_sqrt, bias=res_sh[:])
-        nc.scalar.activation(rabs[:], root[:], ACT.Square)
         nc.scalar.activation(sgn[:], pair[:], ACT.Sign, bias=res_sh[:])
-
-        g = sb([P, I], F32, "g", "v_pool0")
-        u = sb([P, I], F32, "u")
-        nc.gpsimd.tensor_tensor(g[:], psq[:], os_row[:], ALU.mult)
-        nc.gpsimd.tensor_tensor(u[:], tp2[:], tp, ALU.add)
+        nc.scalar.activation(rabs[:], root[:], ACT.Square)
 
         picked1 = pick_on_vector(1)
 
-        aa = sb([P, I], F32, "aa", "v_pool1")
-        bb = sb([P, I], F32, "bb")
+        aa = at(BLOCK, [P, I], F32, "aa")
+        bb = at(BLOCK + ROW, [P, I], F32, "bb")
+        ff = at(BLOCK + 2 * ROW, [P, I], F32, "ff")
         ee = sb([P, I], F32, "ee")
-        ff = sb([P, I], F32, "ff")
         w = sb([P, I], BF16, "w")
         nc.vector.scalar_tensor_tensor(aa[:], ta[:], c[:], sgn[:], ALU.subtract, ALU.mult)
         nc.vector.scalar_tensor_tensor(bb[:], u[:], 0.5, rabs[:], ALU.mult, ALU.mult)
         nc.vector.scalar_tensor_tensor(ff[:], g[:], rz[:], rabs[:], ALU.mult, ALU.mult)
-        halves = [slice(0, I // 2), slice(I // 2, I)]
-        for h in halves:
-            nc.vector.tensor_tensor(ee[:, h], aa[:, h], bb[:, h], ALU.subtract)
-        for h in halves:
-            nc.vector.scalar_tensor_tensor(w[:, h], ee[:, h], 2.0, ff[:, h], ALU.mult, ALU.mult)
+        nc.vector.tensor_tensor(ee[:], aa[:], bb[:], ALU.subtract)
+        nc.vector.scalar_tensor_tensor(w[:], ee[:], 2.0, ff[:], ALU.mult, ALU.mult)
 
-        cast = sb([P, T], BF16, "cast", "pair")
+        cast = sb([P, T], BF16, "cast", "root")
         picked2 = sb([P, I], BF16, "picked2")
         nc.scalar.activation(cast[:], v_pool[2][:], ACT.Copy)
-        v_mx.append(turn_and_quantize(picked1, "v1", "v_pool2", "ff"))
         nc.scalar.activation(picked2[:], cast[:].indirect(idx[:]), ACT.Copy)
         picked3 = pick_on_vector(3, "ee")
-        w_codes, w_scales = turn_and_quantize(w, "w")
-        v_mx.append(turn_and_quantize(picked2, "v2"))
-        v_mx.append(turn_and_quantize(picked3, "v3"))
 
-        def product(blocks, name, evacuate):
-            width = len(blocks) * P
+        w_grouped = sb([P, I], BF16, "w_grouped", "root")
+        v2_grouped = sb([P, I], BF16, "v2_grouped")
+        v3_grouped = sb([P, I], BF16, "v3_grouped")
+        v1_grouped = at(2 * BLOCK, [P, I], BF16, "v1_grouped")
+        turn(w, "w", "a", w_grouped[:])
+        turn(picked1, "v1", "turn1", v1_grouped[:])
+        turn(picked2, "v2", "os_ps", v2_grouped[:])
+        turn(picked3, "v3", "turn0", v3_grouped[:], nc.vector.tensor_copy)
+        v0_mx = quantize(v0_grouped, at(BLOCK + 3 * ROW, [P, P], U32, "v0_codes"), "v0")
+        v1_mx = quantize(v1_grouped, at(3 * BLOCK, [P, P], U32, "v1_codes"), "v1")
+        w_codes, w_scales = quantize(w_grouped, sb([P, P], U32, "w_codes"), "w")
+        v2_mx = quantize(v2_grouped, sb([P, P], U32, "v2_codes"), "v2")
+        v3_mx = quantize(v3_grouped, sb([P, P], U32, "v3_codes"), "v3")
+
+        def product(parts, first, name, evacuate):
+            width = sum(codes.shape[1] for codes, scales in parts)
             acc = psum.tile([P, width], F32, name=name + "_acc")
-            for n, b in enumerate(blocks):
+            start = 0
+            for codes, scales in parts:
                 nc.tensor.matmul_mx(
-                    out=acc[:, n * P : (n + 1) * P], lhsT=w_codes[:].bitcast(FP8X4), lhsT_scale=w_scales[:],
-                    rhs=v_mx[b][0][:].bitcast(FP8X4), rhs_scale=v_mx[b][1][:], start=True, stop=True,
+                    out=acc[:, start : start + codes.shape[1]], lhsT=w_codes[:].bitcast(FP8X4), lhsT_scale=w_scales[:],
+                    rhs=codes[:].bitcast(FP8X4), rhs_scale=scales[:], start=True, stop=True,
                 )
+                start = start + codes.shape[1]
             staged = sb([P, width], F32, name + "_staged")
             evacuate(staged[:], acc[:])
-            nc.sync.dma_start(out[:, blocks[0] * P : blocks[0] * P + width], staged[:])
+            nc.sync.dma_start(out[:, first : first + width], staged[:])
 
-        product([0, 1], "out01", nc.vector.tensor_copy)
-        product([2], "out2", nc.scalar.copy)
-        product([3], "out3", nc.vector.tensor_copy)
+        product([v0_mx, v1_mx], 0, "out01", nc.scalar.copy)
+        product([v2_mx, v3_mx], 2 * P, "out23", nc.vector.tensor_copy)

from contextlib import ExitStack

import concourse.mybir as mybir
from concourse.masks import make_identity

F32 = mybir.dt.float32
BF16 = mybir.dt.bfloat16
I32 = mybir.dt.int32
U32 = mybir.dt.uint32
U16 = mybir.dt.uint16
U8 = mybir.dt.uint8
FP8X4 = mybir.dt.float8_e4m3fn_x4
FP4X4 = mybir.dt.float4_e2m1fn_x4
ALU = mybir.AluOpType
ACT = mybir.ActivationFunctionType
AX = mybir.AxisListType

P = 128
D, E, T, I, Q = 512, 512, 2048, 512, 128
PACK = 4
SPARE = 16
SHIFT_LIMIT = 80.0
BLOCK = 4 * T
ROW = 4 * I
FLOPS = 2 * Q * I * D * 2 + 2 * Q * E * I


def tile_attend_ttneighbourshare_kernel(tc, query, keys_words, keys_scales, reserve, dquery, slot_factor, vals, offs2, offs, out):
    nc = tc.nc
    with ExitStack() as ctx:
        keep = ctx.enter_context(tc.tile_pool(name="keep", bufs=1))
        psum = ctx.enter_context(tc.psum_pool(name="psum", bufs=1))

        reuse = ctx.enter_context(tc.tile_pool(name="reuse", bufs=1))

        def at(offset, shape, dtype, name):
            return reuse.tile(shape, dtype, name=name, offset=offset, align_bytes=64)

        def sb(shape, dtype, name, tag=None):
            return keep.tile(shape, dtype, name=name, tag=tag or name, align_bytes=64)

        idx = keep.tile([P, I // 16], U16, name="idx")
        idx2 = keep.tile([P, I // 16], U16, name="idx2")
        kscale_pool = sb([P, T], U8, "kscale_pool")
        kword_pool = sb([P, T], U16, "kword_pool")
        q_raw = sb([P, PACK, Q], F32, "q_raw")
        dq_raw = sb([P, PACK, Q], F32, "dq_raw")
        v_pool = [at(b * BLOCK, [P, T], F32, "v_pool%d" % b) for b in range(E // P)]
        res_col = sb([P, 1], F32, "res_col")
        os_col = sb([P, PACK], F32, "os_col")

        nc.vector.memset(kscale_pool[:].bitcast(I32), 0)
        nc.sync.dma_start(idx[:], offs)
        nc.sync.dma_start(os_col[:], slot_factor.rearrange("o (p j) -> (o p) j", j=PACK))
        nc.sync.dma_start(kword_pool[:].bitcast(I32), keys_words[0].bitcast(I32))
        nc.sync.dma_start(q_raw[:], query.rearrange("(p j) c -> p j c", j=PACK))
        for quad in range(4):
            nc.sync.dma_start(
                kscale_pool[32 * quad : 32 * quad + 4, :].bitcast(I32),
                keys_scales[0, 4 * quad : 4 * quad + 4, :].bitcast(I32),
            )
        nc.sync.dma_start(dq_raw[:], dquery.rearrange("(p j) c -> p j c", j=PACK))
        nc.sync.dma_start(v_pool[0][:], vals[0:P, :])
        nc.sync.dma_start(idx2[:], offs2)
        nc.sync.dma_start(res_col[:], reserve)
        for b in range(1, E // P):
            nc.sync.dma_start(v_pool[b][:], vals[b * P : (b + 1) * P, :])

        ident = sb([P, P], F32, "ident")
        make_identity(nc, ident[:])
        p_win = sb([P, I + SPARE * 12], F32, "p_win")
        nc.gpsimd.memset(p_win[:, I:], 0.0)
        p = p_win[:, 0:I]

        os_ps = psum.tile([P, PACK, P], F32, name="os_ps", tag="os_ps")
        for j in range(PACK):
            nc.tensor.transpose(os_ps[:, j, :], os_col[:, j : j + 1].to_broadcast([P, P]), ident[:])
        os_row = sb([P, I], F32, "os_row")
        nc.scalar.copy(os_row[:].rearrange("q (n j) -> q n j", j=PACK), os_ps[:].rearrange("q j n -> q n j"))

        halves = [slice(0, I // 2), slice(I // 2, I)]
        list_halves = [slice(0, I // 32), slice(I // 32, I // 16)]

        def quantize_rows(raw, name, codes_tag):
            grouped = sb([P, Q, PACK], BF16, name + "_grouped")
            codes = sb([P, Q], U32, name + "_codes", codes_tag)
            scales = sb([P, Q], U8, name + "_scales")
            nc.scalar.copy(grouped[:], raw[:].rearrange("p j c -> p c j"))
            nc.vector.quantize_mx(out=codes[:].bitcast(FP8X4), scales=scales[:], in_=grouped[:].rearrange("p c j -> p (c j)"))
            return codes, scales

        kwords = sb([P, I], U16, "kwords")
        nc.vector.tensor_copy(kwords[:], kword_pool[:].indirect(idx[:]))
        kscales = [sb([P, I // 2], U8, "kscales0", "kword_pool")]
        nc.vector.tensor_copy(kscales[0][:], kscale_pool[:].indirect(idx[:, list_halves[0]]))
        q_mx = quantize_rows(q_raw, "q", "os_col")
        kscales.append(sb([P, I // 2], U8, "kscales1", "q_grouped"))
        nc.vector.tensor_copy(kscales[1][:], kscale_pool[:].indirect(idx[:, list_halves[1]]))
        dq_mx = quantize_rows(dq_raw, "dq", "kscale_pool")

        def scores(rows_mx, name):
            acc = psum.tile([P, I], F32, name=name, tag=name)
            for h in range(2):
                nc.tensor.matmul_mx(
                    out=acc[:, halves[h]], lhsT=rows_mx[0][:].bitcast(FP8X4), lhsT_scale=rows_mx[1][:],
                    rhs=kwords[:, halves[h]].bitcast(FP4X4), rhs_scale=kscales[h][:], start=True, stop=True,
                )
            return acc

        a = scores(q_mx, "a")
        ta = scores(dq_mx, "ta")

        neg_max = sb([P, 1], F32, "neg_max", "dq_grouped")
        neg_lim = sb([P, 1], F32, "neg_lim")
        shrink = sb([P, 1], F32, "shrink")
        res_sh = sb([P, 1], F32, "res_sh")
        z = sb([P, 1], F32, "z")
        tz = sb([P, 1], F32, "tz")
        c = sb([P, 1], F32, "c")
        nc.vector.tensor_reduce(neg_max[:], a[:], AX.X, ALU.max, negate=True)
        nc.gpsimd.tensor_scalar(neg_lim[:], neg_max[:], SHIFT_LIMIT, -SHIFT_LIMIT, ALU.min, ALU.max)
        nc.scalar.activation(p, a[:], ACT.Exp, bias=neg_max[:], accum_out=z[:])
        psq = sb([P, I], F32, "psq")
        g = sb([P, I], F32, "g")
        nc.scalar.activation(psq[:], p, ACT.Square)
        nc.gpsimd.tensor_tensor(g[:], psq[:], os_row[:], ALU.mult)
        nc.scalar.activation(shrink[:], neg_lim[:], ACT.Exp)
        nc.scalar.activation(res_sh[:], shrink[:], ACT.Copy, scale=res_col[:])

        def turn(src, name, bank, grouped, evacuate=nc.scalar.copy):
            words = src[:].bitcast(F32)
            turned = psum.tile([P, 2, P], F32, name=name + "_turned", tag=bank)
            for h in range(2):
                nc.tensor.transpose(turned[:, h, :], words[:, h : I // 2 : 2], ident[:])
            evacuate(
                grouped.bitcast(F32).rearrange("p (c h) -> p c h", h=2), turned[:].rearrange("p h c -> p c h")
            )

        def quantize(grouped, codes, name):
            scales = sb([P, codes.shape[1]], U8, name + "_scales")
            nc.vector.quantize_mx(out=codes[:].bitcast(FP8X4), scales=scales[:], in_=grouped[:])
            return codes, scales

        def pick_on_vector(b, tag=None):
            picked = sb([P, I], BF16, "picked%d" % b, tag)
            nc.vector.tensor_copy(picked[:], v_pool[b][:].indirect(idx[:]))
            return picked

        picked0 = pick_on_vector(0)
        v0_grouped = sb([P, I], BF16, "v0_grouped", "shrink")
        turn(picked0, "v0", "turn0", v0_grouped[:])

        p2 = at(0, [P, I], F32, "p2")
        rz = at(ROW, [P, 1], F32, "rz")
        tp_win = at(2 * ROW, [P, I + SPARE * 12], F32, "tp_win")
        nc.gpsimd.memset(tp_win[:, I:], 0.0)
        tp = tp_win[:, 0:I]
        pair = sb([P, I], F32, "pair", "psq")
        tp2 = sb([P, I], F32, "tp2")
        u = sb([P, I], F32, "u")
        nc.vector.tensor_copy(p2[:], p_win[:].indirect(idx2[:]))
        nc.vector.scalar_tensor_tensor(tp, ta[:], 1.0, p, ALU.mult, ALU.mult, accum_out=tz[:])
        nc.gpsimd.tensor_tensor(pair[:], p2[:], p, ALU.add)
        nc.vector.tensor_copy(tp2[:], tp_win[:].indirect(idx2[:]))
        nc.gpsimd.tensor_tensor(u[:], tp2[:], tp, ALU.add)
        nc.vector.reciprocal(rz[:], z[:])
        nc.vector.tensor_scalar(c[:], tz[:], rz[:], 0.5, ALU.mult, ALU.mult)

        root = sb([P, I], F32, "root")
        rabs = sb([P, I], F32, "rabs")
        sgn = sb([P, I], F32, "sgn")
        nc.scalar.activation(root[:], pair[:], ACT.Abs_reciprocal_sqrt, bias=res_sh[:])
        nc.scalar.activation(sgn[:], pair[:], ACT.Sign, bias=res_sh[:])
        nc.scalar.activation(rabs[:], root[:], ACT.Square)

        picked1 = pick_on_vector(1)

        aa = at(BLOCK, [P, I], F32, "aa")
        bb = at(BLOCK + ROW, [P, I], F32, "bb")
        ff = at(BLOCK + 2 * ROW, [P, I], F32, "ff")
        ee = sb([P, I], F32, "ee")
        w = sb([P, I], BF16, "w")
        nc.vector.scalar_tensor_tensor(aa[:], ta[:], c[:], sgn[:], ALU.subtract, ALU.mult)
        nc.vector.scalar_tensor_tensor(bb[:], u[:], 0.5, rabs[:], ALU.mult, ALU.mult)
        nc.vector.scalar_tensor_tensor(ff[:], g[:], rz[:], rabs[:], ALU.mult, ALU.mult)
        nc.vector.tensor_tensor(ee[:], aa[:], bb[:], ALU.subtract)
        nc.vector.scalar_tensor_tensor(w[:], ee[:], 2.0, ff[:], ALU.mult, ALU.mult)

        cast = sb([P, T], BF16, "cast", "root")
        picked2 = sb([P, I], BF16, "picked2")
        nc.scalar.activation(cast[:], v_pool[2][:], ACT.Copy)
        nc.scalar.activation(picked2[:], cast[:].indirect(idx[:]), ACT.Copy)
        picked3 = pick_on_vector(3, "ee")

        w_grouped = sb([P, I], BF16, "w_grouped", "root")
        v2_grouped = sb([P, I], BF16, "v2_grouped")
        v3_grouped = sb([P, I], BF16, "v3_grouped")
        v1_grouped = at(2 * BLOCK, [P, I], BF16, "v1_grouped")
        turn(w, "w", "a", w_grouped[:])
        turn(picked1, "v1", "turn1", v1_grouped[:])
        turn(picked2, "v2", "os_ps", v2_grouped[:])
        turn(picked3, "v3", "turn0", v3_grouped[:], nc.vector.tensor_copy)
        v0_mx = quantize(v0_grouped, at(BLOCK + 3 * ROW, [P, P], U32, "v0_codes"), "v0")
        v1_mx = quantize(v1_grouped, at(3 * BLOCK, [P, P], U32, "v1_codes"), "v1")
        w_codes, w_scales = quantize(w_grouped, sb([P, P], U32, "w_codes"), "w")
        v2_mx = quantize(v2_grouped, sb([P, P], U32, "v2_codes"), "v2")
        v3_mx = quantize(v3_grouped, sb([P, P], U32, "v3_codes"), "v3")

        def product(parts, first, name, evacuate):
            width = sum(codes.shape[1] for codes, scales in parts)
            acc = psum.tile([P, width], F32, name=name + "_acc")
            start = 0
            for codes, scales in parts:
                nc.tensor.matmul_mx(
                    out=acc[:, start : start + codes.shape[1]], lhsT=w_codes[:].bitcast(FP8X4), lhsT_scale=w_scales[:],
                    rhs=codes[:].bitcast(FP8X4), rhs_scale=scales[:], start=True, stop=True,
                )
                start = start + codes.shape[1]
            staged = sb([P, width], F32, name + "_staged")
            evacuate(staged[:], acc[:])
            nc.sync.dma_start(out[:, first : first + width], staged[:])

        product([v0_mx, v1_mx], 0, "out01", nc.scalar.copy)
        product([v2_mx, v3_mx], 2 * P, "out23", nc.vector.tensor_copy)
